import numpy as np, ml_dtypes
CORES = [242,247,114,119]
N = 4
import mx_ref
NC, G = 128, 2
C = np.float32(0.0145)
BF = ml_dtypes.bfloat16
def cut(t, i, w=512):
    return t[:, w * i:w * i + w]
def tile(rs):
    return np.stack(rs, axis=2).reshape(128, -1).astype(BF)
def layer(w, X):
    out = []
    for i in range(G):
        for t in range(len(X)):
            p = mx_ref.matmul(mx_ref.quantize(cut(w, len(X) * i + t)), X[t])
            z = p if t == 0 else z + p
        out.append(z)
    return out
def act(Z):
    return [np.maximum(s * z, 0) * C for z in Z for s in (1, -1)]
def setup_inputs(rng):
    def f(*shape):
        return mx_ref.flush((rng.standard_normal(shape, dtype=np.float32) * np.exp2(rng.integers(-2, 3, shape[:-1] + (1,)))).astype(BF))
    return {"x": f(N, 128, 4 * NC), "w1": f(N, 128, G * N * 512), "w2": f(N, 128, 512)}
def setup_inputs_blocks(rng):
    d = setup_inputs(rng)
    for k in ("x", "w1", "w2"): d[k] = mx_ref.spread(d[k], rng, 4)
    return d
def setup_inputs_wide(rng):
    d = setup_inputs(rng)
    for k in ("x", "w1", "w2"): d[k] = mx_ref.flush((d[k].astype(np.float32) * np.exp2(rng.integers(-6, 7, (N, 1, 1))).astype(np.float32)).astype(BF))
    return d
def reference(x, w1, w2, own=None):
    X = [mx_ref.quantize(x[j]) for j in range(N)]
    h = np.stack([tile(act(layer(w1[r], X))) for r in range(N)])
    use = h if own is None else own["h"]
    H = [mx_ref.quantize(use[j]) for j in range(N)]
    y = np.zeros((N, 128, N * NC), np.float32)
    for r in range(N):
        qw = mx_ref.quantize(w2[r])
        for j in range(N):
            y[r][:, NC * j:NC * j + NC] = mx_ref.matmul(qw, H[j])
    return {"h": h, "y": y}

from concourse.bass import DstId, RemoteDMATransfer
from concourse.mybir import dt, AluOpType, ActivationFunctionType

N, G = 4, 2
NC, TW = 128, 512
BANK = 512
C = 0.0145

SCRATCH = {
    "xb": ("sbuf", [128, TW], "bfloat16"),
    "w1b": ("sbuf", [128, G * N * TW], "bfloat16"),
    "w2b": ("sbuf", [128, TW], "bfloat16"),
    "hb": ("sbuf", [128, TW], "bfloat16"),
    "ysb": ("sbuf", [128, N * NC], "float32"),
    "xq": ("sbuf", [128, N * NC], "float8_e4m3fn_x4"),
    "xs": ("sbuf", [128, N * NC], "uint8"),
    "w1q": ("sbuf", [128, G * N * NC], "float8_e4m3fn_x4"),
    "w1s": ("sbuf", [128, G * N * NC], "uint8"),
    "w2q": ("sbuf", [128, NC], "float8_e4m3fn_x4"),
    "w2s": ("sbuf", [128, NC], "uint8"),
    "hq": ("sbuf", [128, N * NC], "float8_e4m3fn_x4"),
    "hs": ("sbuf", [128, N * NC], "uint8"),
    "z": ("psum", [128, G * BANK], "float32"),
    "yp": ("psum", [128, N * BANK], "float32"),
}
SEMAPHORES = (["ldx", "go", "ldv", "qx", "qv", "qh", "av", "asc", "sndx", "sndh", "sts", "stc"]
              + ["ldw%d" % p for p in range(2 * G)] + ["qw%d" % p for p in range(2 * G)]
              + ["z%d" % i for i in range(G)]
              + [n % j for n in ("xa%d", "ha%d", "ym%d", "yc%d") for j in range(N)])


def _bits(m):
    return [e for e in range(m.bit_length()) if (m >> e) & 1]


def _mask(es):
    m = 0
    for e in es:
        m |= 1 << e
    return m


def _runs(js):
    out = []
    for j in sorted(js):
        if out and out[-1][0] + out[-1][1] == j:
            out[-1][1] += 1
        else:
            out.append([j, 1])
    return out


def _plan(r, cores, topo):
    me = cores[r]
    near = [j for j in range(N) if j != r and (topo.host(cores[j]), topo.chip(cores[j])) == (topo.host(me), topo.chip(me))]
    far = [j for j in range(N) if j != r and j not in near]
    far.sort(key=lambda j: topo.die(cores[j]) != topo.die(me))
    leave = _bits(min(topo.mask(me, cores[j]) for j in far))
    stay = [e for e in _bits(min(topo.mask(me, cores[j]) for j in near)) if e not in leave]
    eng = {}
    for js, es in ((far, leave), (near, stay)):
        n = len(es) // len(js)
        for t, j in enumerate(js):
            eng[j] = es[n * t:n * t + n]
    return near, far, eng


def rank_program(g, core, T, topo):
    r = T.rank_of(core)
    if r is None:
        return
    S, cores = T.sem, T.cores
    ve, te, sc, sy = g.vector, g.tensor, g.scalar, g.sync
    near, far, eng = _plan(r, cores, topo)
    lands = {j: 2 * len(_plan(j, cores, topo)[2][r]) for j in near + far}
    leaves = 2 * sum(len(eng[j]) for j in near + far)

    def slot(t, j, n=1):
        return t[:, NC * j:NC * (j + n)]

    sy.dma_start(T.xb[:, :], T.x[:, :]).then_inc(S.ldx, 16)
    sy.sem_inc(S.go, 1)
    sc.wait_ge(S.go, 1)
    pieces = [(i, j0, n) for js in ([r] + near, far) for i in range(G) for j0, n in _runs(js)]
    piece_of = {}
    for p, (i, j0, n) in enumerate(pieces):
        k = N * i + j0
        q = (sy, sc)[p % 2]
        q.dma_start(T.w1b[:, TW * k:TW * (k + n)], T.w1[:, TW * k:TW * (k + n)]).then_inc(S["ldw%d" % p], 16)
        for j in range(j0, j0 + n):
            piece_of[(i, j)] = p
    sy.wait_ge(S.sndx, leaves)
    sy.dma_start(T.w2b[:, :], T.w2[:, :]).then_inc(S.ldv, 16)

    def send(js, codes, plane, name, left):
        for pick in (lambda: slot(codes, r).bitcast(dt.uint8), lambda: slot(plane, r)):
            trs = []
            for j in js:
                rid, pid = topo.addr(cores[j], core)
                trs.append(RemoteDMATransfer(dst_ids=[DstId(rid=rid, pnc=pid)], dma_engine_mask=_mask(eng[j]),
                                             remote_sem=S[name % r], src=pick(), dst=pick()))
            g.remote_dma_fused(trs, local_sem=left)

    g.wait_ge(S.qx, 1)
    send(far, T.xq, T.xs, "xa%d", S.sndx)
    send(near, T.xq, T.xs, "xa%d", S.sndx)
    g.wait_ge(S.qh, 1)
    send(far + near, T.hq, T.hs, "ha%d", S.sndh)

    ve.wait_ge(S.ldx, 16)
    ve.quantize_mx(slot(T.xq, r), slot(T.xs, r), T.xb[:, :]).then_inc(S.qx, 1)
    for p, (i, j0, n) in enumerate(pieces):
        k = N * i + j0
        ve.wait_ge(S["ldw%d" % p], 16)
        ve.quantize_mx(slot(T.w1q, k, n), slot(T.w1s, k, n), T.w1b[:, TW * k:TW * (k + n)]).then_inc(S["qw%d" % p], 1)
    ve.wait_ge(S.z0, 1)
    for b, s in ((0, C), (1, -C)):
        ve.tensor_scalar(T.hb[:, b:TW:4], T.z[:, 0:NC], s, 0.0, AluOpType.mult, AluOpType.max).then_inc(S.av, 1)
    ve.wait_ge(S.av, 2)
    ve.wait_ge(S.asc, 2)
    ve.quantize_mx(slot(T.hq, r), slot(T.hs, r), T.hb[:, :]).then_inc(S.qh, 1)
    ve.wait_ge(S.ldv, 16)
    ve.quantize_mx(T.w2q[:, :], T.w2s[:, :], T.w2b[:, :]).then_inc(S.qv, 1)

    sc.wait_ge(S.z1, 1)
    for b, s in ((2, C), (3, -C)):
        sc.activation(T.hb[:, b:TW:4], T.z[:, BANK:BANK + NC], ActivationFunctionType.Relu, scale=s).then_inc(S.asc, 1)

    order = [r] + near + far
    seen = set()

    def need(sem, val):
        if sem not in seen:
            seen.add(sem)
            te.wait_ge(S[sem], val)

    for j in order:
        for i in range(G):
            k = N * i + j
            need("qw%d" % piece_of[(i, j)], 1)
            if j == r:
                need("qx", 1)
            else:
                need("xa%d" % j, lands[j])
            mm = te.matmul_mx(T.z[:, BANK * i:BANK * i + NC], slot(T.w1q, k), slot(T.w1s, k), slot(T.xq, j), slot(T.xs, j),
                              j == order[0], j == order[-1])
            if j == order[-1]:
                mm.then_inc(S["z%d" % i], 1)

    need("qh", 1)
    need("qv", 1)
    for t, j in enumerate(order):
        if j != r:
            need("ha%d" % j, lands[j])
        bank = T.yp[:, BANK * j:BANK * j + NC]
        te.matmul_mx(bank, T.w2q[:, :], T.w2s[:, :], slot(T.hq, j), slot(T.hs, j), True, True).then_inc(S["ym%d" % j], 1)
        if t % 2 == 0:
            ve.wait_ge(S["ym%d" % j], 1)
            ve.tensor_copy(slot(T.ysb, j), bank).then_inc(S["yc%d" % j], 1)
        else:
            sc.wait_ge(S["ym%d" % j], 1)
            sc.activation(slot(T.ysb, j), bank, ActivationFunctionType.Copy).then_inc(S["yc%d" % j], 1)
        if j == ([r] + near)[-1]:
            for jj in [r] + near:
                sc.wait_ge(S["yc%d" % jj], 1)
            stc = 0
            for j0, n in _runs([r] + near):
                sc.dma_start(slot(T.y, j0, n), slot(T.ysb, j0, n)).then_inc(S.stc, 16)
                stc += 16

    sy.wait_ge(S.av, 2)
    sy.wait_ge(S.asc, 2)
    sy.wait_ge(S.sndh, leaves)
    sy.dma_start(T.h[:, :], T.hb[:, :]).then_inc(S.sts, 16)
    sts = 16
    for j in far:
        sy.wait_ge(S["yc%d" % j], 1)
    for j0, n in _runs(far):
        sy.dma_start(slot(T.y, j0, n), slot(T.ysb, j0, n)).then_inc(S.sts, 16)
        sts += 16
    sy.wait_ge(S.sts, sts)
    sc.wait_ge(S.stc, stc)
